import numpy as np
import ml_dtypes


def mxq(x, axis, fmt="e4m3"):
    dtype, down = {"e4m3": (ml_dtypes.float8_e4m3fn, 7), "e5m2": (ml_dtypes.float8_e5m2, 14)}[fmt]
    v = np.moveaxis(np.asarray(x, np.float32).astype(ml_dtypes.bfloat16).astype(np.float64), axis, -1)
    blocks = v.reshape(v.shape[:-1] + (-1, 32))
    amax = np.abs(blocks).max(-1, keepdims=True)
    byte = np.maximum(np.where(amax > 0, np.frexp(amax)[1] - 1 + 127, 0) - down, 1)
    scale = np.exp2(byte - 127.0)
    codes = (blocks / scale).astype(np.float32).astype(dtype).astype(np.float64)
    return np.moveaxis((codes * scale).reshape(v.shape), -1, axis)


WIDE = False


def mx_kscale(k):
    if not WIDE:
        return np.ones(k)
    levels = np.array([10, -10, 5, -5, 0])
    if k % 512:
        return np.exp2(np.random.permutation(np.resize(levels, k // 32))).repeat(32)
    a = np.empty((k // 512, 16))
    for p in range(k // 512):
        a[p, :8] = np.random.permutation(np.resize(levels, 8))
        for g in range(8):
            far = levels[np.abs(levels - a[p, g]) >= 10]
            a[p, g + 8] = far[np.random.randint(len(far))]
    return np.exp2(a.ravel()).repeat(32)


def f64(x):
    return np.asarray(x).astype(np.float64)


def striped8(idx):
    return np.asarray(idx).reshape(8, -1, 16).transpose(0, 2, 1).reshape(128, -1).astype(np.uint16)


def unstriped8(offs):
    return offs.reshape(8, 16, -1).transpose(0, 2, 1).reshape(8, -1).astype(np.int64)


def pick8(x, idx, run):
    r = np.arange(len(x))
    return x[r[:, None], idx[r % (8 * run) // run]]


E2M1 = np.array([0.0, 0.5, 1.0, 1.5, 2.0, 3.0, 4.0, 6.0, -0.0, -0.5, -1.0, -1.5, -2.0, -3.0, -4.0, -6.0])


def pack_weight(w, fmt):
    k, n = w.shape
    w = f64(np.asarray(w, np.float32).astype(ml_dtypes.bfloat16)).reshape(k // 32, 32, n)
    amax = np.abs(w).max(1)
    if fmt == "e4m3":
        byte = np.frexp(amax)[1] - 1 + 127 - 7
    else:
        mant, ex = np.frexp(amax / 6.0)
        byte = np.where(mant > 0.5, ex, ex - 1) + 127
    byte = np.clip(np.where(amax > 0, byte, 1), 1, 254)
    scaled = (w * np.exp2(127.0 - byte)[:, None, :]).reshape(k, n).astype(np.float32)
    by_word = np.ascontiguousarray(scaled.reshape(k // 512, 128, 4, n).transpose(0, 1, 3, 2))
    if fmt == "e4m3":
        words = by_word.astype(ml_dtypes.float8_e4m3fn).view(np.uint8)
    else:
        c = by_word.astype(ml_dtypes.float4_e2m1fn).view(np.uint8) & 0xF
        words = (c[..., 0::2] | (c[..., 1::2] << 4)).reshape(k // 512, 128, 2 * n)
    return np.ascontiguousarray(words), np.ascontiguousarray(byte.astype(np.uint8).reshape(k // 512, 16, n))


def unpack_weight(words, scales, fmt):
    g, _, n = scales.shape
    words = np.ascontiguousarray(words).reshape(g, 128, n, -1)
    if fmt == "e4m3":
        vals = words.view(ml_dtypes.float8_e4m3fn).astype(np.float64)
    else:
        nib = np.empty((g, 128, n, 4), np.uint8)
        nib[..., 0::2] = words & 0xF
        nib[..., 1::2] = words >> 4
        vals = E2M1[nib]
    vals = vals * np.repeat(np.exp2(scales.astype(np.float64) - 127.0), 8, axis=1)[..., None]
    return vals.transpose(0, 1, 3, 2).reshape(g * 512, n)


D, K, T, U, X, I, J, Q = 512, 512, 1024, 1024, 1024, 512, 256, 128


def setup_inputs():
    n = np.random.standard_normal
    idx = np.stack([np.random.permutation(T)[:I] for _ in range(8)])
    idx2 = np.stack([np.random.permutation(U)[:I] for _ in range(8)])
    idx3 = np.stack([np.random.permutation(I)[:J] for _ in range(8)])
    idx4 = np.stack([np.random.permutation(X)[:J] for _ in range(8)])
    idx5 = np.stack([np.random.permutation(U)[:J] for _ in range(8)])
    idx6 = np.stack([np.random.permutation(X)[:I] for _ in range(8)])
    idx7 = np.stack([np.random.permutation(U)[:I] for _ in range(8)])
    fd = mx_kscale(D)
    fk = mx_kscale(K)
    wqp = pack_weight(n((D, K)) * 1.0 / np.sqrt(D) * fd[:, None] * fk, "e4m3")
    cachep = pack_weight(n((K, T)) * 1.0 / np.sqrt(K) / fk[:, None], "e4m3")
    draftp = pack_weight(n((K, U)) * 1.0 / np.sqrt(K) / fk[:, None], "e2m1")
    archp = pack_weight(n((D, X)) * 1.0 / np.sqrt(D) * fd[:, None], "e4m3")
    return {
        "states": (n((D, Q)) * 0.95 / fd[:, None]).astype(np.float32),
        "wq_words": wqp[0],
        "wq_scales": wqp[1],
        "cache_words": cachep[0],
        "cache_scales": cachep[1],
        "draft_words": draftp[0],
        "draft_scales": draftp[1],
        "arch_words": archp[0],
        "arch_scales": archp[1],
        "offs": striped8(idx),
        "offs2": striped8(idx2),
        "offs3": striped8(idx3),
        "offs4": striped8(idx4),
        "offs5": striped8(idx5),
        "offs6": striped8(idx6),
        "offs7": striped8(idx7),
    }


def reference(states, wq_words, wq_scales, cache_words, cache_scales, draft_words, draft_scales, arch_words, arch_scales, offs, offs2, offs3, offs4, offs5, offs6, offs7):
    idx = unstriped8(offs)
    idx2 = unstriped8(offs2)
    idx3 = unstriped8(offs3)
    idx4 = unstriped8(offs4)
    idx5 = unstriped8(offs5)
    idx6 = unstriped8(offs6)
    idx7 = unstriped8(offs7)
    wqu = unpack_weight(wq_words, wq_scales, "e4m3")
    cacheu = unpack_weight(cache_words, cache_scales, "e4m3")
    draftu = unpack_weight(draft_words, draft_scales, "e2m1")
    archu = unpack_weight(arch_words, arch_scales, "e4m3")
    statesq = mxq(f64(states), 0, "e4m3")
    qv = wqu.T @ statesq
    qvq = mxq(qv, 0, "e4m3")
    a = qvq.T @ cacheu
    b = qvq.T @ draftu
    c0 = statesq.T @ archu
    w = pick8(a, idx, 16) + pick8(b, idx2, 16)
    v = pick8(w, idx3, 16) * 1.5
    f1 = np.zeros((Q, X))
    f1[np.arange(Q)[:, None], idx4[np.arange(Q) % 128 // 16]] = v
    f2 = np.zeros((Q, U))
    f2[np.arange(Q)[:, None], idx5[np.arange(Q) % 128 // 16]] = v
    cc = c0 - f1
    bb = np.maximum(b, f2)
    y = pick8(cc, idx6, 16) + pick8(bb, idx7, 16)
    return y

@@ -1,0 +1,189 @@
+from contextlib import ExitStack
+
+import concourse.mybir as mybir
+
+D, K, T, U, X, I, J, Q = 512, 512, 1024, 1024, 1024, 512, 256, 128
+
+FLOPS = 2 * D * K * Q + 2 * K * Q * T + 2 * K * Q * U + 2 * D * Q * X
+
+F32 = mybir.dt.float32
+BF16 = mybir.dt.bfloat16
+I32 = mybir.dt.int32
+U32 = mybir.dt.uint32
+U16 = mybir.dt.uint16
+U8 = mybir.dt.uint8
+FP8X4 = mybir.dt.float8_e4m3fn_x4
+FP4X4 = mybir.dt.float4_e2m1fn_x4
+ALU = mybir.AluOpType
+COPY = mybir.ActivationFunctionType.Copy
+
+P = 128
+PACK = 4
+BANK = 512
+GROUP = 16
+
+
+def tile_attend_slotpages_sidethree_kernel(
+    tc, states, wq_words, wq_scales, cache_words, cache_scales, draft_words, draft_scales,
+    arch_words, arch_scales, offs, offs2, offs3, offs4, offs5, offs6, offs7, out,
+):
+    nc = tc.nc
+    with ExitStack() as ctx:
+        sb = ctx.enter_context(tc.tile_pool(name="sb", bufs=1))
+        ps = ctx.enter_context(tc.psum_pool(name="ps", bufs=1))
+
+        def plane_tile(name, n):
+            t = sb.tile([P, 2 * n], U8, name=name, align_bytes=64)
+            nc.vector.memset(t[:, 0:n].bitcast(I32), 0)
+            return t
+
+        def load_scales(t, scales):
+            rows = scales[0].bitcast(I32).rearrange("(g h j) n -> g j h n", g=2, h=2)
+            view = t[:].bitcast(I32).rearrange("p (h n) -> p h n", h=2)
+            for g in range(2):
+                nc.sync.dma_start(view[64 * g : 64 * g + 4], rows[g])
+
+        def spread_scales(t, n):
+            view = t[:].bitcast(I32)
+            for g in range(2):
+                nc.vector.tensor_copy(
+                    view[64 * g + 32 : 64 * g + 36, 0 : n // 4], view[64 * g : 64 * g + 4, n // 4 : n // 2]
+                )
+
+        def load_words(name, words2d):
+            src = words2d.bitcast(I32)
+            t = sb.tile([P, src.shape[1]], I32, name=name, align_bytes=256)
+            nc.sync.dma_start(t[:], src)
+            return t
+
+        def load_list(name, src):
+            t = sb.tile([P, src.shape[1]], U16, name=name)
+            nc.sync.dma_start(t[:], src)
+            return t
+
+        cache_plane = plane_tile("cache_plane", T)
+        draft_plane = plane_tile("draft_plane", U)
+        wq_plane = sb.tile([P, K], U8, name="wq_plane", align_bytes=64)
+        nc.vector.memset(wq_plane[:].bitcast(I32), 0)
+        arch_plane = plane_tile("arch_plane", X)
+        f2 = sb.tile([P, U], F32, name="f2")
+        f1 = sb.tile([P, X], F32, name="f1")
+        nc.gpsimd.memset(f2[:], 0.0)
+        nc.gpsimd.memset(f1[:], 0.0)
+
+        wq_stage = sb.tile([PACK, 4, K // 4], I32, name="wq_stage")
+        nc.sync.dma_start(wq_stage[:], wq_scales[0].bitcast(I32).rearrange("(g j) n -> j g n", g=4))
+        st_raw = sb.tile([P, PACK, Q], F32, name="st_raw", align_bytes=256)
+        nc.sync.dma_start(st_raw[:], states.rearrange("(p j) q -> p j q", j=PACK))
+        wq_raw = load_words("wq_raw", wq_words[0].rearrange("p n t -> p (n t)"))
+        load_scales(cache_plane, cache_scales)
+        load_scales(draft_plane, draft_scales)
+        cache_w = load_words("cache_w", cache_words[0].rearrange("p n t -> p (n t)"))
+        draft_w = load_words("draft_w", draft_words[0])
+        l1 = load_list("l1", offs)
+        l2 = load_list("l2", offs2)
+        l3 = load_list("l3", offs3)
+        load_scales(arch_plane, arch_scales)
+        arch_w = load_words("arch_w", arch_words[0].rearrange("p n t -> p (n t)"))
+        l4 = load_list("l4", offs4)
+        l5 = load_list("l5", offs5)
+        l7 = load_list("l7", offs7)
+        l6 = load_list("l6", offs6)
+
+        st_bf = sb.tile([P, Q, PACK], BF16, name="st_bf", align_bytes=64)
+        nc.scalar.activation(st_bf[:], st_raw[:].rearrange("p j q -> p q j"), COPY)
+        for g in range(4):
+            nc.vector.tensor_copy(wq_plane[32 * g : 32 * g + 4, :].bitcast(I32), wq_stage[:, g, :])
+        wq_sc = sb.tile([P, PACK, P], U8, name="wq_sc", align_bytes=64)
+        nc.vector.tensor_copy(wq_sc[:], wq_plane[:].rearrange("p (m t) -> p t m", t=PACK))
+        wq_w = sb.tile([P, PACK, P], U32, name="wq_w", align_bytes=64)
+        dealt = wq_raw[:].bitcast(U32).rearrange("p (m t) -> p t m", t=PACK)
+        nc.vector.tensor_copy(wq_w[:, 0:2, :].bitcast(I32), wq_raw[:].rearrange("p (m t) -> p t m", t=PACK)[:, 0:2, :])
+        nc.scalar.copy(wq_w[:, 2:4, :], dealt[:, 2:4, :])
+        st_codes = sb.tile([P, Q], U32, name="st_codes", align_bytes=64)
+        st_sc = sb.tile([P, Q], U8, name="st_sc", align_bytes=64)
+        nc.vector.quantize_mx(st_codes[:].bitcast(FP8X4), st_sc[:], st_bf[:].rearrange("p q j -> p (q j)"))
+
+        qv_ps = ps.tile([P, PACK, Q], F32, name="qv_ps", tag="bank7")
+        for t in range(PACK):
+            nc.tensor.matmul_mx(
+                qv_ps[:, t, :], lhsT=wq_w[:, t, :].bitcast(FP8X4), lhsT_scale=wq_sc[:, t, :],
+                rhs=st_codes[:].bitcast(FP8X4), rhs_scale=st_sc[:], start=True, stop=True,
+            )
+
+        def scores(name, codes, sc, words, plane, fmt, n, first_bank):
+            banks = []
+            pieces = plane.shape[1] // 2 // n
+            per = words.shape[1] // pieces
+            for h in range(pieces):
+                bank = ps.tile([P, n], F32, name=name + str(h), tag="bank%d" % (first_bank + h))
+                nc.tensor.matmul_mx(
+                    bank[:], lhsT=codes[:].bitcast(FP8X4), lhsT_scale=sc[:],
+                    rhs=words[:, h * per : (h + 1) * per].bitcast(fmt),
+                    rhs_scale=plane[:, h * n : (h + 1) * n], start=True, stop=True,
+                )
+                banks.append(bank)
+            return banks
+
+        qv_bf = sb.tile([P, Q, PACK], BF16, name="qv_bf", align_bytes=64)
+        nc.scalar.copy(qv_bf[:], qv_ps[:].rearrange("p t q -> p q t"))
+        spread_scales(cache_plane, T)
+        spread_scales(draft_plane, U)
+        qv_codes = sb.tile([P, Q], U32, name="qv_codes", align_bytes=64)
+        qv_sc = sb.tile([P, Q], U8, name="qv_sc", align_bytes=64)
+        nc.vector.quantize_mx(qv_codes[:].bitcast(FP8X4), qv_sc[:], qv_bf[:].rearrange("p q t -> p (q t)"))
+
+        n = BANK // 2
+        a_ps = scores("a_ps", qv_codes, qv_sc, cache_w, cache_plane, FP8X4, n, 0)
+        b_ps = scores("b_ps", qv_codes, qv_sc, draft_w, draft_plane, FP4X4, n, 4)
+
+        a = sb.tile([P, T], F32, name="a")
+        b = sb.tile([P, U], F32, name="b")
+        for h in range(4):
+            if h % 2 == 0:
+                nc.scalar.copy(a[:, h * n : (h + 1) * n], a_ps[h][:])
+            else:
+                nc.vector.tensor_copy(a[:, h * n : (h + 1) * n], a_ps[h][:])
+        for h in range(4):
+            nc.vector.tensor_copy(b[:, h * n : (h + 1) * n], b_ps[h][:])
+
+        half = I // 2
+        hc = half // GROUP
+        ga = sb.tile([P, I], F32, name="ga")
+        w = sb.tile([P, I], F32, name="w")
+        for h in range(2):
+            nc.scalar.activation(ga[:, h * half : (h + 1) * half], a[:].indirect(l1[:, h * hc : (h + 1) * hc]), COPY)
+        gb1 = sb.tile([P, half], F32, name="gb1")
+        nc.scalar.activation(gb1[:], b[:].indirect(l2[:, hc : 2 * hc]), COPY)
+        nc.vector.tensor_tensor(w[:, 0:half], b[:].indirect(l2[:, 0:hc]), ga[:, 0:half], ALU.add)
+        nc.vector.tensor_tensor(w[:, half:I], ga[:, half:I], gb1[:], ALU.add)
+        v = sb.tile([P, J], F32, name="v")
+        for h in range(2):
+            nc.vector.tensor_scalar(
+                v[:, h * 128 : (h + 1) * 128], w[:].indirect(l3[:, h * 8 : (h + 1) * 8]), 1.5, 0.0, ALU.mult, ALU.add
+            )
+
+        nc.scalar.activation(f1[:].indirect(l4[:, 0:4]), v[:, 0:64], COPY)
+        nc.scalar.activation(f2[:].indirect(l5[:]), v[:], COPY)
+        nc.scalar.activation(f1[:].indirect(l4[:, 4:16]), v[:, 64:J], COPY)
+
+        spread_scales(arch_plane, X)
+        c0_ps = scores("c0_ps", st_codes, st_sc, arch_w, arch_plane, FP8X4, BANK, 0)
+
+        bb = sb.tile([P, U], F32, name="bb")
+        nc.vector.tensor_tensor(bb[:], b[:], f2[:], ALU.max)
+        cc = sb.tile([P, X], F32, name="cc")
+        for h in range(2):
+            nc.vector.tensor_tensor(
+                cc[:, h * BANK : (h + 1) * BANK], c0_ps[h][:], f1[:, h * BANK : (h + 1) * BANK], ALU.subtract
+            )
+        gb = sb.tile([P, I], F32, name="gb")
+        res = sb.tile([P, I], F32, name="res")
+        for h in range(2):
+            nc.scalar.activation(gb[:, h * half : (h + 1) * half], bb[:].indirect(l7[:, h * hc : (h + 1) * hc]), COPY)
+        gc1 = sb.tile([P, half], F32, name="gc1")
+        nc.scalar.activation(gc1[:], cc[:].indirect(l6[:, hc : 2 * hc]), COPY)
+        nc.vector.tensor_tensor(res[:, 0:half], cc[:].indirect(l6[:, 0:hc]), gb[:, 0:half], ALU.add)
+        nc.sync.dma_start(out[:, 0:half], res[:, 0:half])
+        nc.vector.tensor_tensor(res[:, half:I], gb[:, half:I], gc1[:], ALU.add)
+        nc.sync.dma_start(out[:, half:I], res[:, half:I])

@@ -67,9 +67,9 @@ def tile_attend_slotpages_sidethree_kernel(
         nc.vector.memset(wq_plane[:].bitcast(I32), 0)
         arch_plane = plane_tile("arch_plane", X)
         f2 = sb.tile([P, U], F32, name="f2")
-        f1 = sb.tile([P, X], F32, name="f1")
-        nc.gpsimd.memset(f2[:], 0.0)
-        nc.gpsimd.memset(f1[:], 0.0)
+        nc.vector.memset(f2[:], 0.0)
+        factor = sb.tile([P, 1], F32, name="factor")
+        nc.vector.memset(factor[:], 1.5)
 
         wq_stage = sb.tile([PACK, 4, K // 4], I32, name="wq_stage")
         nc.sync.dma_start(wq_stage[:], wq_scales[0].bitcast(I32).rearrange("(g j) n -> j g n", g=4))
@@ -85,24 +85,26 @@ def tile_attend_slotpages_sidethree_kernel(
         l3 = load_list("l3", offs3)
         load_scales(arch_plane, arch_scales)
         arch_w = load_words("arch_w", arch_words[0].rearrange("p n t -> p (n t)"))
-        l4 = load_list("l4", offs4)
         l5 = load_list("l5", offs5)
+        l4 = load_list("l4", offs4)
         l7 = load_list("l7", offs7)
         l6 = load_list("l6", offs6)
 
         st_bf = sb.tile([P, Q, PACK], BF16, name="st_bf", align_bytes=64)
-        nc.scalar.activation(st_bf[:], st_raw[:].rearrange("p j q -> p q j"), COPY)
+        woven = st_raw[:].rearrange("p j q -> p q j")
+        nc.scalar.activation(st_bf[:, Q // 2 : Q, :], woven[:, Q // 2 : Q, :], COPY)
         for g in range(4):
             nc.vector.tensor_copy(wq_plane[32 * g : 32 * g + 4, :].bitcast(I32), wq_stage[:, g, :])
         wq_sc = sb.tile([P, PACK, P], U8, name="wq_sc", align_bytes=64)
         nc.vector.tensor_copy(wq_sc[:], wq_plane[:].rearrange("p (m t) -> p t m", t=PACK))
+        nc.vector.tensor_copy(st_bf[:, 0 : Q // 2, :], woven[:, 0 : Q // 2, :])
+        st_codes = sb.tile([P, Q], U32, name="st_codes", align_bytes=64)
+        st_sc = sb.tile([P, Q], U8, name="st_sc", align_bytes=64)
+        nc.vector.quantize_mx(st_codes[:].bitcast(FP8X4), st_sc[:], st_bf[:].rearrange("p q j -> p (q j)"))
         wq_w = sb.tile([P, PACK, P], U32, name="wq_w", align_bytes=64)
         dealt = wq_raw[:].bitcast(U32).rearrange("p (m t) -> p t m", t=PACK)
         nc.vector.tensor_copy(wq_w[:, 0:2, :].bitcast(I32), wq_raw[:].rearrange("p (m t) -> p t m", t=PACK)[:, 0:2, :])
         nc.scalar.copy(wq_w[:, 2:4, :], dealt[:, 2:4, :])
-        st_codes = sb.tile([P, Q], U32, name="st_codes", align_bytes=64)
-        st_sc = sb.tile([P, Q], U8, name="st_sc", align_bytes=64)
-        nc.vector.quantize_mx(st_codes[:].bitcast(FP8X4), st_sc[:], st_bf[:].rearrange("p q j -> p (q j)"))
 
         qv_ps = ps.tile([P, PACK, Q], F32, name="qv_ps", tag="bank7")
         for t in range(PACK):
@@ -145,27 +147,25 @@ def tile_attend_slotpages_sidethree_kernel(
             else:
                 nc.vector.tensor_copy(a[:, h * n : (h + 1) * n], a_ps[h][:])
         for h in range(4):
-            nc.vector.tensor_copy(b[:, h * n : (h + 1) * n], b_ps[h][:])
+            nc.scalar.copy(b[:, h * n : (h + 1) * n], b_ps[h][:])
 
         half = I // 2
         hc = half // GROUP
         ga = sb.tile([P, I], F32, name="ga")
-        w = sb.tile([P, I], F32, name="w")
-        for h in range(2):
-            nc.scalar.activation(ga[:, h * half : (h + 1) * half], a[:].indirect(l1[:, h * hc : (h + 1) * hc]), COPY)
+        w = sb.tile([P, I], F32, name="w", tag="w_then_f1")
+        nc.vector.tensor_copy(ga[:], a[:].indirect(l1[:]))
         gb1 = sb.tile([P, half], F32, name="gb1")
         nc.scalar.activation(gb1[:], b[:].indirect(l2[:, hc : 2 * hc]), COPY)
         nc.vector.tensor_tensor(w[:, 0:half], b[:].indirect(l2[:, 0:hc]), ga[:, 0:half], ALU.add)
         nc.vector.tensor_tensor(w[:, half:I], ga[:, half:I], gb1[:], ALU.add)
         v = sb.tile([P, J], F32, name="v")
-        for h in range(2):
-            nc.vector.tensor_scalar(
-                v[:, h * 128 : (h + 1) * 128], w[:].indirect(l3[:, h * 8 : (h + 1) * 8]), 1.5, 0.0, ALU.mult, ALU.add
-            )
+        nc.vector.tensor_scalar(v[:, 0:128], w[:].indirect(l3[:, 0:8]), 1.5, 0.0, ALU.mult, ALU.add)
+        nc.scalar.activation(v[:, 128:256], w[:].indirect(l3[:, 8:16]), COPY, scale=factor[:])
 
-        nc.scalar.activation(f1[:].indirect(l4[:, 0:4]), v[:, 0:64], COPY)
         nc.scalar.activation(f2[:].indirect(l5[:]), v[:], COPY)
-        nc.scalar.activation(f1[:].indirect(l4[:, 4:16]), v[:, 64:J], COPY)
+        f1 = sb.tile([P, X], F32, name="f1", tag="w_then_f1")
+        nc.vector.memset(f1[:], 0.0)
+        nc.scalar.activation(f1[:].indirect(l4[:]), v[:], COPY)
 
         spread_scales(arch_plane, X)
         c0_ps = scores("c0_ps", st_codes, st_sc, arch_w, arch_plane, FP8X4, BANK, 0)

@@ -19,8 +19,14 @@ COPY = mybir.ActivationFunctionType.Copy
 
 P = 128
 PACK = 4
+QUADS = 4
+QUAD = P // QUADS
+LIVE = 4
+HEAD = 16
 BANK = 512
-GROUP = 16
+PIECE = 256
+PICK_FACTOR = 1.5
+RUN = 4
 
 
 def tile_attend_slotpages_sidethree_kernel(
@@ -32,56 +38,74 @@ def tile_attend_slotpages_sidethree_kernel(
         sb = ctx.enter_context(tc.tile_pool(name="sb", bufs=1))
         ps = ctx.enter_context(tc.psum_pool(name="ps", bufs=1))
 
-        def plane_tile(name, n):
-            t = sb.tile([P, 2 * n], U8, name=name, align_bytes=64)
-            nc.vector.memset(t[:, 0:n].bitcast(I32), 0)
-            return t
+        def plane_with_spare(name, n, engine):
+            tile = sb.tile([P, 2 * n], U8, name=name, align_bytes=64)
+            engine.memset(tile[:, 0:n].bitcast(I32), 0)
+            return tile
 
-        def load_scales(t, scales):
+        def load_scales(tile, scales):
             rows = scales[0].bitcast(I32).rearrange("(g h j) n -> g j h n", g=2, h=2)
-            view = t[:].bitcast(I32).rearrange("p (h n) -> p h n", h=2)
+            view = tile[:].bitcast(I32).rearrange("p (h n) -> p h n", h=2)
             for g in range(2):
-                nc.sync.dma_start(view[64 * g : 64 * g + 4], rows[g])
+                nc.sync.dma_start(view[2 * QUAD * g : 2 * QUAD * g + LIVE], rows[g])
 
-        def spread_scales(t, n):
-            view = t[:].bitcast(I32)
+        def spread_scales(tile, n):
+            view = tile[:].bitcast(I32)
             for g in range(2):
+                low = 2 * QUAD * g
                 nc.vector.tensor_copy(
-                    view[64 * g + 32 : 64 * g + 36, 0 : n // 4], view[64 * g : 64 * g + 4, n // 4 : n // 2]
+                    view[low + QUAD : low + QUAD + LIVE, 0 : n // 4], view[low : low + LIVE, n // 4 : n // 2]
                 )
 
-        def load_words(name, words2d):
-            src = words2d.bitcast(I32)
-            t = sb.tile([P, src.shape[1]], I32, name=name, align_bytes=256)
-            nc.sync.dma_start(t[:], src)
-            return t
+        def load_words(name, raw):
+            src = raw.bitcast(I32)
+            tile = sb.tile([P, src.shape[1]], I32, name=name, align_bytes=256)
+            nc.sync.dma_start(tile[:], src)
+            return tile
 
         def load_list(name, src):
-            t = sb.tile([P, src.shape[1]], U16, name=name)
-            nc.sync.dma_start(t[:], src)
-            return t
+            tile = sb.tile([P, src.shape[1]], U16, name=name)
+            nc.sync.dma_start(tile[:], src)
+            return tile
 
-        cache_plane = plane_tile("cache_plane", T)
-        draft_plane = plane_tile("draft_plane", U)
+        def quantise(name, values):
+            codes = sb.tile([P, Q], U32, name=name + "_codes", align_bytes=64)
+            plane = sb.tile([P, Q], U8, name=name + "_plane", align_bytes=64)
+            nc.vector.quantize_mx(codes[:].bitcast(FP8X4), plane[:], values[:].rearrange("p q t -> p (q t)"))
+            return codes, plane
+
+        def score(name, rows, words, plane, bank):
+            tile = ps.tile([P, plane.shape[1]], F32, name=name, tag="bank%d" % bank)
+            nc.tensor.matmul_mx(
+                tile[:], lhsT=rows[0][:].bitcast(FP8X4), lhsT_scale=rows[1][:], rhs=words, rhs_scale=plane,
+                start=True, stop=True,
+            )
+            return tile
+
+        draft_plane = plane_with_spare("draft_plane", U, nc.vector)
+        cache_plane = plane_with_spare("cache_plane", T, nc.gpsimd)
         wq_plane = sb.tile([P, K], U8, name="wq_plane", align_bytes=64)
         nc.vector.memset(wq_plane[:].bitcast(I32), 0)
-        arch_plane = plane_tile("arch_plane", X)
+        arch_plane = plane_with_spare("arch_plane", X, nc.vector)
         f2 = sb.tile([P, U], F32, name="f2")
         nc.vector.memset(f2[:], 0.0)
         factor = sb.tile([P, 1], F32, name="factor")
-        nc.vector.memset(factor[:], 1.5)
+        nc.vector.memset(factor[:], PICK_FACTOR)
 
-        wq_stage = sb.tile([PACK, 4, K // 4], I32, name="wq_stage")
-        nc.sync.dma_start(wq_stage[:], wq_scales[0].bitcast(I32).rearrange("(g j) n -> j g n", g=4))
+        wq_stage = sb.tile([LIVE, QUADS, K // 4], I32, name="wq_stage")
+        nc.sync.dma_start(wq_stage[:], wq_scales[0].bitcast(I32).rearrange("(g j) n -> j g n", g=QUADS))
         st_raw = sb.tile([P, PACK, Q], F32, name="st_raw", align_bytes=256)
         nc.sync.dma_start(st_raw[:], states.rearrange("(p j) q -> p j q", j=PACK))
         wq_raw = load_words("wq_raw", wq_words[0].rearrange("p n t -> p (n t)"))
-        load_scales(cache_plane, cache_scales)
         load_scales(draft_plane, draft_scales)
-        cache_w = load_words("cache_w", cache_words[0].rearrange("p n t -> p (n t)"))
+        load_scales(cache_plane, cache_scales)
         draft_w = load_words("draft_w", draft_words[0])
-        l1 = load_list("l1", offs)
+        cache_flat = cache_words[0].rearrange("p n t -> p (n t)")
+        cache_w = [
+            load_words("cache_w%d" % h, cache_flat[:, h * PACK * BANK : (h + 1) * PACK * BANK]) for h in range(2)
+        ]
         l2 = load_list("l2", offs2)
+        l1 = load_list("l1", offs)
         l3 = load_list("l3", offs3)
         load_scales(arch_plane, arch_scales)
         arch_w = load_words("arch_w", arch_words[0].rearrange("p n t -> p (n t)"))
@@ -91,76 +115,80 @@ def tile_attend_slotpages_sidethree_kernel(
         l6 = load_list("l6", offs6)
 
         st_bf = sb.tile([P, Q, PACK], BF16, name="st_bf", align_bytes=64)
-        woven = st_raw[:].rearrange("p j q -> p q j")
-        nc.scalar.activation(st_bf[:, Q // 2 : Q, :], woven[:, Q // 2 : Q, :], COPY)
-        for g in range(4):
-            nc.vector.tensor_copy(wq_plane[32 * g : 32 * g + 4, :].bitcast(I32), wq_stage[:, g, :])
+        st_in = st_raw[:].rearrange("p j (c i) -> p c j i", i=RUN)
+        st_out = st_bf[:].rearrange("p (c i) j -> p c j i", i=RUN)
+        runs = Q // RUN
+        nc.scalar.activation(st_out[:, runs // 2 : runs], st_in[:, runs // 2 : runs], COPY)
+
+        for g in range(QUADS):
+            nc.vector.tensor_copy(wq_plane[QUAD * g : QUAD * g + LIVE, :].bitcast(I32), wq_stage[:, g, :])
         wq_sc = sb.tile([P, PACK, P], U8, name="wq_sc", align_bytes=64)
         nc.vector.tensor_copy(wq_sc[:], wq_plane[:].rearrange("p (m t) -> p t m", t=PACK))
-        nc.vector.tensor_copy(st_bf[:, 0 : Q // 2, :], woven[:, 0 : Q // 2, :])
-        st_codes = sb.tile([P, Q], U32, name="st_codes", align_bytes=64)
-        st_sc = sb.tile([P, Q], U8, name="st_sc", align_bytes=64)
-        nc.vector.quantize_mx(st_codes[:].bitcast(FP8X4), st_sc[:], st_bf[:].rearrange("p q j -> p (q j)"))
+        nc.vector.tensor_copy(st_out[:, 0 : runs // 2], st_in[:, 0 : runs // 2])
+        st_q = quantise("st", st_bf)
         wq_w = sb.tile([P, PACK, P], U32, name="wq_w", align_bytes=64)
-        dealt = wq_raw[:].bitcast(U32).rearrange("p (m t) -> p t m", t=PACK)
-        nc.vector.tensor_copy(wq_w[:, 0:2, :].bitcast(I32), wq_raw[:].rearrange("p (m t) -> p t m", t=PACK)[:, 0:2, :])
-        nc.scalar.copy(wq_w[:, 2:4, :], dealt[:, 2:4, :])
+        nc.vector.tensor_copy(
+            wq_w[:].bitcast(I32).rearrange("p t m -> p m t")[:, :, 0 : PACK // 2],
+            wq_raw[:].rearrange("p (m t) -> p m t", t=PACK)[:, :, 0 : PACK // 2],
+        )
+        nc.scalar.copy(
+            wq_w[:].rearrange("p t m -> p m t")[:, :, PACK // 2 : PACK],
+            wq_raw[:].bitcast(U32).rearrange("p (m t) -> p m t", t=PACK)[:, :, PACK // 2 : PACK],
+        )
 
-        qv_ps = ps.tile([P, PACK, Q], F32, name="qv_ps", tag="bank7")
+        pieces = T // PIECE
+        qv_ps = ps.tile([P, PACK, Q], F32, name="qv_ps", tag="bank%d" % (2 * pieces - 1))
         for t in range(PACK):
             nc.tensor.matmul_mx(
                 qv_ps[:, t, :], lhsT=wq_w[:, t, :].bitcast(FP8X4), lhsT_scale=wq_sc[:, t, :],
-                rhs=st_codes[:].bitcast(FP8X4), rhs_scale=st_sc[:], start=True, stop=True,
+                rhs=st_q[0][:].bitcast(FP8X4), rhs_scale=st_q[1][:], start=True, stop=True,
             )
-
-        def scores(name, codes, sc, words, plane, fmt, n, first_bank):
-            banks = []
-            pieces = plane.shape[1] // 2 // n
-            per = words.shape[1] // pieces
-            for h in range(pieces):
-                bank = ps.tile([P, n], F32, name=name + str(h), tag="bank%d" % (first_bank + h))
-                nc.tensor.matmul_mx(
-                    bank[:], lhsT=codes[:].bitcast(FP8X4), lhsT_scale=sc[:],
-                    rhs=words[:, h * per : (h + 1) * per].bitcast(fmt),
-                    rhs_scale=plane[:, h * n : (h + 1) * n], start=True, stop=True,
-                )
-                banks.append(bank)
-            return banks
-
         qv_bf = sb.tile([P, Q, PACK], BF16, name="qv_bf", align_bytes=64)
         nc.scalar.copy(qv_bf[:], qv_ps[:].rearrange("p t q -> p q t"))
-        spread_scales(cache_plane, T)
         spread_scales(draft_plane, U)
-        qv_codes = sb.tile([P, Q], U32, name="qv_codes", align_bytes=64)
-        qv_sc = sb.tile([P, Q], U8, name="qv_sc", align_bytes=64)
-        nc.vector.quantize_mx(qv_codes[:].bitcast(FP8X4), qv_sc[:], qv_bf[:].rearrange("p q t -> p (q t)"))
+        spread_scales(cache_plane, T)
+        qv_q = quantise("qv", qv_bf)
 
-        n = BANK // 2
-        a_ps = scores("a_ps", qv_codes, qv_sc, cache_w, cache_plane, FP8X4, n, 0)
-        b_ps = scores("b_ps", qv_codes, qv_sc, draft_w, draft_plane, FP4X4, n, 4)
+        b_ps = [
+            score("b_ps%d" % h, qv_q, draft_w[:, h * PIECE // 2 : (h + 1) * PIECE // 2].bitcast(FP4X4),
+                  draft_plane[:, h * PIECE : (h + 1) * PIECE], h)
+            for h in range(pieces)
+        ]
+        a_ps = [
+            score("a_ps%d" % h, qv_q, cache_w[h // 2][:, h % 2 * PIECE : (h % 2 + 1) * PIECE].bitcast(FP8X4),
+                  cache_plane[:, h * PIECE : (h + 1) * PIECE], pieces + h)
+            for h in range(pieces)
+        ]
 
         a = sb.tile([P, T], F32, name="a")
         b = sb.tile([P, U], F32, name="b")
-        for h in range(4):
-            if h % 2 == 0:
-                nc.scalar.copy(a[:, h * n : (h + 1) * n], a_ps[h][:])
+        for h in range(pieces):
+            if h % 2 == 1:
+                nc.scalar.copy(b[:, h * PIECE : (h + 1) * PIECE], b_ps[h][:])
             else:
-                nc.vector.tensor_copy(a[:, h * n : (h + 1) * n], a_ps[h][:])
-        for h in range(4):
-            nc.scalar.copy(b[:, h * n : (h + 1) * n], b_ps[h][:])
+                nc.vector.tensor_copy(b[:, h * PIECE : (h + 1) * PIECE], b_ps[h][:])
+        for h in range(pieces):
+            nc.scalar.copy(a[:, h * PIECE : (h + 1) * PIECE], a_ps[h][:])
 
-        half = I // 2
-        hc = half // GROUP
-        ga = sb.tile([P, I], F32, name="ga")
+        def gather_add(name, dst, window, lst, other):
+            half = I // 2
+            cols = half // HEAD
+            upper = sb.tile([P, half], F32, name=name)
+            nc.scalar.activation(upper[:], window[:].indirect(lst[:, cols : 2 * cols]), COPY)
+            nc.vector.tensor_tensor(dst[:, 0:half], window[:].indirect(lst[:, 0:cols]), other[:, 0:half], ALU.add)
+            nc.vector.tensor_tensor(dst[:, half:I], other[:, half:I], upper[:], ALU.add)
+            return slice(0, half), slice(half, I)
+
+        b_picked = sb.tile([P, I], F32, name="b_picked")
         w = sb.tile([P, I], F32, name="w", tag="w_then_f1")
-        nc.vector.tensor_copy(ga[:], a[:].indirect(l1[:]))
-        gb1 = sb.tile([P, half], F32, name="gb1")
-        nc.scalar.activation(gb1[:], b[:].indirect(l2[:, hc : 2 * hc]), COPY)
-        nc.vector.tensor_tensor(w[:, 0:half], b[:].indirect(l2[:, 0:hc]), ga[:, 0:half], ALU.add)
-        nc.vector.tensor_tensor(w[:, half:I], ga[:, half:I], gb1[:], ALU.add)
+        nc.vector.tensor_copy(b_picked[:], b[:].indirect(l2[:]))
+        gather_add("a_upper", w, a, l1, b_picked)
+
         v = sb.tile([P, J], F32, name="v")
-        nc.vector.tensor_scalar(v[:, 0:128], w[:].indirect(l3[:, 0:8]), 1.5, 0.0, ALU.mult, ALU.add)
-        nc.scalar.activation(v[:, 128:256], w[:].indirect(l3[:, 8:16]), COPY, scale=factor[:])
+        picks = J // 2
+        pick_cols = picks // HEAD
+        nc.vector.tensor_scalar(v[:, 0:picks], w[:].indirect(l3[:, 0:pick_cols]), PICK_FACTOR, 0.0, ALU.mult, ALU.add)
+        nc.scalar.activation(v[:, picks:J], w[:].indirect(l3[:, pick_cols : 2 * pick_cols]), COPY, scale=factor[:])
 
         nc.scalar.activation(f2[:].indirect(l5[:]), v[:], COPY)
         f1 = sb.tile([P, X], F32, name="f1", tag="w_then_f1")
@@ -168,22 +196,25 @@ def tile_attend_slotpages_sidethree_kernel(
         nc.scalar.activation(f1[:].indirect(l4[:]), v[:], COPY)
 
         spread_scales(arch_plane, X)
-        c0_ps = scores("c0_ps", st_codes, st_sc, arch_w, arch_plane, FP8X4, BANK, 0)
+        c0_ps = [
+            score("c0_ps%d" % h, st_q, arch_w[:, h * BANK : (h + 1) * BANK].bitcast(FP8X4),
+                  arch_plane[:, h * BANK : (h + 1) * BANK], h)
+            for h in range(X // BANK)
+        ]
 
         bb = sb.tile([P, U], F32, name="bb")
         nc.vector.tensor_tensor(bb[:], b[:], f2[:], ALU.max)
         cc = sb.tile([P, X], F32, name="cc")
-        for h in range(2):
-            nc.vector.tensor_tensor(
-                cc[:, h * BANK : (h + 1) * BANK], c0_ps[h][:], f1[:, h * BANK : (h + 1) * BANK], ALU.subtract
-            )
-        gb = sb.tile([P, I], F32, name="gb")
+        for h in range(X // BANK):
+            cols = slice(h * BANK, (h + 1) * BANK)
+            nc.vector.tensor_tensor(cc[:, cols], c0_ps[h][:], f1[:, cols], ALU.subtract)
+
+        bb_picked = sb.tile([P, I], F32, name="bb_picked")
         res = sb.tile([P, I], F32, name="res")
         for h in range(2):
-            nc.scalar.activation(gb[:, h * half : (h + 1) * half], bb[:].indirect(l7[:, h * hc : (h + 1) * hc]), COPY)
-        gc1 = sb.tile([P, half], F32, name="gc1")
-        nc.scalar.activation(gc1[:], cc[:].indirect(l6[:, hc : 2 * hc]), COPY)
-        nc.vector.tensor_tensor(res[:, 0:half], cc[:].indirect(l6[:, 0:hc]), gb[:, 0:half], ALU.add)
-        nc.sync.dma_start(out[:, 0:half], res[:, 0:half])
-        nc.vector.tensor_tensor(res[:, half:I], gb[:, half:I], gc1[:], ALU.add)
-        nc.sync.dma_start(out[:, half:I], res[:, half:I])
+            n = I // 2
+            nc.scalar.activation(
+                bb_picked[:, h * n : (h + 1) * n], bb[:].indirect(l7[:, h * n // HEAD : (h + 1) * n // HEAD]), COPY
+            )
+        for cols in gather_add("cc_upper", res, cc, l6, bb_picked):
+            nc.sync.dma_start(out[:, cols], res[:, cols])

from contextlib import ExitStack

import concourse.mybir as mybir

D, K, T, U, X, I, J, Q = 512, 512, 1024, 1024, 1024, 512, 256, 128

FLOPS = 2 * D * K * Q + 2 * K * Q * T + 2 * K * Q * U + 2 * D * Q * X

F32 = mybir.dt.float32
BF16 = mybir.dt.bfloat16
I32 = mybir.dt.int32
U32 = mybir.dt.uint32
U16 = mybir.dt.uint16
U8 = mybir.dt.uint8
FP8X4 = mybir.dt.float8_e4m3fn_x4
FP4X4 = mybir.dt.float4_e2m1fn_x4
ALU = mybir.AluOpType
COPY = mybir.ActivationFunctionType.Copy

P = 128
PACK = 4
QUADS = 4
QUAD = P // QUADS
LIVE = 4
HEAD = 16
BANK = 512
PIECE = 256
PICK_FACTOR = 1.5
RUN = 4


def tile_attend_slotpages_sidethree_kernel(
    tc, states, wq_words, wq_scales, cache_words, cache_scales, draft_words, draft_scales,
    arch_words, arch_scales, offs, offs2, offs3, offs4, offs5, offs6, offs7, out,
):
    nc = tc.nc
    with ExitStack() as ctx:
        sb = ctx.enter_context(tc.tile_pool(name="sb", bufs=1))
        ps = ctx.enter_context(tc.psum_pool(name="ps", bufs=1))

        def plane_with_spare(name, n, engine):
            tile = sb.tile([P, 2 * n], U8, name=name, align_bytes=64)
            engine.memset(tile[:, 0:n].bitcast(I32), 0)
            return tile

        def load_scales(tile, scales):
            rows = scales[0].bitcast(I32).rearrange("(g h j) n -> g j h n", g=2, h=2)
            view = tile[:].bitcast(I32).rearrange("p (h n) -> p h n", h=2)
            for g in range(2):
                nc.sync.dma_start(view[2 * QUAD * g : 2 * QUAD * g + LIVE], rows[g])

        def spread_scales(tile, n):
            view = tile[:].bitcast(I32)
            for g in range(2):
                low = 2 * QUAD * g
                nc.vector.tensor_copy(
                    view[low + QUAD : low + QUAD + LIVE, 0 : n // 4], view[low : low + LIVE, n // 4 : n // 2]
                )

        def load_words(name, raw):
            src = raw.bitcast(I32)
            tile = sb.tile([P, src.shape[1]], I32, name=name, align_bytes=256)
            nc.sync.dma_start(tile[:], src)
            return tile

        def load_list(name, src):
            tile = sb.tile([P, src.shape[1]], U16, name=name)
            nc.sync.dma_start(tile[:], src)
            return tile

        def quantise(name, values):
            codes = sb.tile([P, Q], U32, name=name + "_codes", align_bytes=64)
            plane = sb.tile([P, Q], U8, name=name + "_plane", align_bytes=64)
            nc.vector.quantize_mx(codes[:].bitcast(FP8X4), plane[:], values[:].rearrange("p q t -> p (q t)"))
            return codes, plane

        def score(name, rows, words, plane, bank):
            tile = ps.tile([P, plane.shape[1]], F32, name=name, tag="bank%d" % bank)
            nc.tensor.matmul_mx(
                tile[:], lhsT=rows[0][:].bitcast(FP8X4), lhsT_scale=rows[1][:], rhs=words, rhs_scale=plane,
                start=True, stop=True,
            )
            return tile

        draft_plane = plane_with_spare("draft_plane", U, nc.vector)
        cache_plane = plane_with_spare("cache_plane", T, nc.gpsimd)
        wq_plane = sb.tile([P, K], U8, name="wq_plane", align_bytes=64)
        nc.vector.memset(wq_plane[:].bitcast(I32), 0)
        arch_plane = plane_with_spare("arch_plane", X, nc.vector)
        f2 = sb.tile([P, U], F32, name="f2")
        nc.vector.memset(f2[:], 0.0)
        factor = sb.tile([P, 1], F32, name="factor")
        nc.vector.memset(factor[:], PICK_FACTOR)

        wq_stage = sb.tile([LIVE, QUADS, K // 4], I32, name="wq_stage")
        nc.sync.dma_start(wq_stage[:], wq_scales[0].bitcast(I32).rearrange("(g j) n -> j g n", g=QUADS))
        st_raw = sb.tile([P, PACK, Q], F32, name="st_raw", align_bytes=256)
        nc.sync.dma_start(st_raw[:], states.rearrange("(p j) q -> p j q", j=PACK))
        wq_raw = load_words("wq_raw", wq_words[0].rearrange("p n t -> p (n t)"))
        load_scales(draft_plane, draft_scales)
        load_scales(cache_plane, cache_scales)
        draft_w = load_words("draft_w", draft_words[0])
        cache_flat = cache_words[0].rearrange("p n t -> p (n t)")
        cache_w = [
            load_words("cache_w%d" % h, cache_flat[:, h * PACK * BANK : (h + 1) * PACK * BANK]) for h in range(2)
        ]
        l2 = load_list("l2", offs2)
        l1 = load_list("l1", offs)
        l3 = load_list("l3", offs3)
        load_scales(arch_plane, arch_scales)
        arch_w = load_words("arch_w", arch_words[0].rearrange("p n t -> p (n t)"))
        l5 = load_list("l5", offs5)
        l4 = load_list("l4", offs4)
        l7 = load_list("l7", offs7)
        l6 = load_list("l6", offs6)

        st_bf = sb.tile([P, Q, PACK], BF16, name="st_bf", align_bytes=64)
        st_in = st_raw[:].rearrange("p j (c i) -> p c j i", i=RUN)
        st_out = st_bf[:].rearrange("p (c i) j -> p c j i", i=RUN)
        runs = Q // RUN
        nc.scalar.activation(st_out[:, runs // 2 : runs], st_in[:, runs // 2 : runs], COPY)

        for g in range(QUADS):
            nc.vector.tensor_copy(wq_plane[QUAD * g : QUAD * g + LIVE, :].bitcast(I32), wq_stage[:, g, :])
        wq_sc = sb.tile([P, PACK, P], U8, name="wq_sc", align_bytes=64)
        nc.vector.tensor_copy(wq_sc[:], wq_plane[:].rearrange("p (m t) -> p t m", t=PACK))
        nc.vector.tensor_copy(st_out[:, 0 : runs // 2], st_in[:, 0 : runs // 2])
        st_q = quantise("st", st_bf)
        wq_w = sb.tile([P, PACK, P], U32, name="wq_w", align_bytes=64)
        nc.vector.tensor_copy(
            wq_w[:].bitcast(I32).rearrange("p t m -> p m t")[:, :, 0 : PACK // 2],
            wq_raw[:].rearrange("p (m t) -> p m t", t=PACK)[:, :, 0 : PACK // 2],
        )
        nc.scalar.copy(
            wq_w[:].rearrange("p t m -> p m t")[:, :, PACK // 2 : PACK],
            wq_raw[:].bitcast(U32).rearrange("p (m t) -> p m t", t=PACK)[:, :, PACK // 2 : PACK],
        )

        pieces = T // PIECE
        qv_ps = ps.tile([P, PACK, Q], F32, name="qv_ps", tag="bank%d" % (2 * pieces - 1))
        for t in range(PACK):
            nc.tensor.matmul_mx(
                qv_ps[:, t, :], lhsT=wq_w[:, t, :].bitcast(FP8X4), lhsT_scale=wq_sc[:, t, :],
                rhs=st_q[0][:].bitcast(FP8X4), rhs_scale=st_q[1][:], start=True, stop=True,
            )
        qv_bf = sb.tile([P, Q, PACK], BF16, name="qv_bf", align_bytes=64)
        nc.scalar.copy(qv_bf[:], qv_ps[:].rearrange("p t q -> p q t"))
        spread_scales(draft_plane, U)
        spread_scales(cache_plane, T)
        qv_q = quantise("qv", qv_bf)

        b_ps = [
            score("b_ps%d" % h, qv_q, draft_w[:, h * PIECE // 2 : (h + 1) * PIECE // 2].bitcast(FP4X4),
                  draft_plane[:, h * PIECE : (h + 1) * PIECE], h)
            for h in range(pieces)
        ]
        a_ps = [
            score("a_ps%d" % h, qv_q, cache_w[h // 2][:, h % 2 * PIECE : (h % 2 + 1) * PIECE].bitcast(FP8X4),
                  cache_plane[:, h * PIECE : (h + 1) * PIECE], pieces + h)
            for h in range(pieces)
        ]

        a = sb.tile([P, T], F32, name="a")
        b = sb.tile([P, U], F32, name="b")
        for h in range(pieces):
            if h % 2 == 1:
                nc.scalar.copy(b[:, h * PIECE : (h + 1) * PIECE], b_ps[h][:])
            else:
                nc.vector.tensor_copy(b[:, h * PIECE : (h + 1) * PIECE], b_ps[h][:])
        for h in range(pieces):
            nc.scalar.copy(a[:, h * PIECE : (h + 1) * PIECE], a_ps[h][:])

        def gather_add(name, dst, window, lst, other):
            half = I // 2
            cols = half // HEAD
            upper = sb.tile([P, half], F32, name=name)
            nc.scalar.activation(upper[:], window[:].indirect(lst[:, cols : 2 * cols]), COPY)
            nc.vector.tensor_tensor(dst[:, 0:half], window[:].indirect(lst[:, 0:cols]), other[:, 0:half], ALU.add)
            nc.vector.tensor_tensor(dst[:, half:I], other[:, half:I], upper[:], ALU.add)
            return slice(0, half), slice(half, I)

        b_picked = sb.tile([P, I], F32, name="b_picked")
        w = sb.tile([P, I], F32, name="w", tag="w_then_f1")
        nc.vector.tensor_copy(b_picked[:], b[:].indirect(l2[:]))
        gather_add("a_upper", w, a, l1, b_picked)

        v = sb.tile([P, J], F32, name="v")
        picks = J // 2
        pick_cols = picks // HEAD
        nc.vector.tensor_scalar(v[:, 0:picks], w[:].indirect(l3[:, 0:pick_cols]), PICK_FACTOR, 0.0, ALU.mult, ALU.add)
        nc.scalar.activation(v[:, picks:J], w[:].indirect(l3[:, pick_cols : 2 * pick_cols]), COPY, scale=factor[:])

        nc.scalar.activation(f2[:].indirect(l5[:]), v[:], COPY)
        f1 = sb.tile([P, X], F32, name="f1", tag="w_then_f1")
        nc.vector.memset(f1[:], 0.0)
        nc.scalar.activation(f1[:].indirect(l4[:]), v[:], COPY)

        spread_scales(arch_plane, X)
        c0_ps = [
            score("c0_ps%d" % h, st_q, arch_w[:, h * BANK : (h + 1) * BANK].bitcast(FP8X4),
                  arch_plane[:, h * BANK : (h + 1) * BANK], h)
            for h in range(X // BANK)
        ]

        bb = sb.tile([P, U], F32, name="bb")
        nc.vector.tensor_tensor(bb[:], b[:], f2[:], ALU.max)
        cc = sb.tile([P, X], F32, name="cc")
        for h in range(X // BANK):
            cols = slice(h * BANK, (h + 1) * BANK)
            nc.vector.tensor_tensor(cc[:, cols], c0_ps[h][:], f1[:, cols], ALU.subtract)

        bb_picked = sb.tile([P, I], F32, name="bb_picked")
        res = sb.tile([P, I], F32, name="res")
        for h in range(2):
            n = I // 2
            nc.scalar.activation(
                bb_picked[:, h * n : (h + 1) * n], bb[:].indirect(l7[:, h * n // HEAD : (h + 1) * n // HEAD]), COPY
            )
        for cols in gather_add("cc_upper", res, cc, l6, bb_picked):
            nc.sync.dma_start(out[:, cols], res[:, cols])
